import numpy as np
import ml_dtypes


def mxq(x, axis, fmt="e4m3"):
    dtype, down = {"e4m3": (ml_dtypes.float8_e4m3fn, 7), "e5m2": (ml_dtypes.float8_e5m2, 14)}[fmt]
    v = np.moveaxis(np.asarray(x, np.float32).astype(ml_dtypes.bfloat16).astype(np.float64), axis, -1)
    blocks = v.reshape(v.shape[:-1] + (-1, 32))
    amax = np.abs(blocks).max(-1, keepdims=True)
    byte = np.maximum(np.where(amax > 0, np.frexp(amax)[1] - 1 + 127, 0) - down, 1)
    scale = np.exp2(byte - 127.0)
    codes = (blocks / scale).astype(np.float32).astype(dtype).astype(np.float64)
    return np.moveaxis((codes * scale).reshape(v.shape), -1, axis)


WIDE = False


def mx_kscale(k, group=512):
    if not WIDE:
        return np.ones(k)
    levels = np.array([10, -10, 5, -5, 0])
    if group != 512:
        return np.exp2(np.random.permutation(np.resize(levels, k // group))).repeat(group)
    if k % 512:
        return np.exp2(np.random.permutation(np.resize(levels, k // 32))).repeat(32)
    a = np.empty((k // 512, 16))
    for p in range(k // 512):
        a[p, :8] = np.random.permutation(np.resize(levels, 8))
        for g in range(8):
            far = levels[np.abs(levels - a[p, g]) >= 10]
            a[p, g + 8] = far[np.random.randint(len(far))]
    return np.exp2(a.ravel()).repeat(32)


def f64(x):
    return np.asarray(x).astype(np.float64)


def sigmoid(v):
    return 1.0 / (1.0 + np.exp(-v))


def bf(x):
    return np.asarray(x, np.float32).astype(ml_dtypes.bfloat16)


def planes(Y):
    r, m = Y.shape
    b = f64(bf(Y)).reshape(r // 32, 32, m)
    amax = np.abs(b).max(1)
    byte = np.clip(np.where(amax > 0, np.frexp(amax)[1] - 1 + 127 - 7, 1), 1, 254)
    codes = (b * np.exp2(127.0 - byte)[:, None, :]).reshape(r, m).astype(np.float32).astype(ml_dtypes.float8_e4m3fn).view(np.uint8)
    words = codes.reshape(r // 512, 128, 4, m).transpose(0, 1, 3, 2)
    return np.ascontiguousarray(words), np.ascontiguousarray(byte.astype(np.uint8).reshape(r // 512, 16, m))


G, D, M, N = 2, 256, 256, 512


def setup_inputs():
    n = np.random.standard_normal
    s_d = mx_kscale(D, 0)
    return {
        "x": (n((G, D, N)) * s_d[:, None]).astype(np.float32),
        "w1": (n((G, D, M)) / np.sqrt(D) / s_d[:, None]).astype(np.float32),
        "w2": (n((G, D, M)) / np.sqrt(D) / s_d[:, None]).astype(np.float32),
        "gn": (np.random.uniform(0.5, 2.0, (G, M, 1))).astype(np.float32),
        "dx": (n((G, D, N)) * s_d[:, None]).astype(np.float32),
        "og": (np.random.uniform(0.5, 2.0, (G, M, 1))).astype(np.float32),
        "base": (0.3 * n((G, M, N))).astype(np.float32),
    }


def reference(x, w1, w2, gn, dx, og, base):
    w1q = mxq(f64(w1), 1, "e4m3")
    xq = mxq(f64(x), 1, "e4m3")
    z1 = w1q.transpose(0, 2, 1) @ xq
    dxq = mxq(f64(dx), 1, "e4m3")
    tz1 = w1q.transpose(0, 2, 1) @ dxq
    w2q = mxq(f64(w2), 1, "e4m3")
    z2 = w2q.transpose(0, 2, 1) @ xq
    tz2 = w2q.transpose(0, 2, 1) @ dxq
    rm = np.sqrt(np.mean(np.square(z1), axis=-1, keepdims=True) + 0.01)
    nz = z1 / rm * f64(gn)
    xrm = np.mean(tz1 * z1 * 2.0, axis=-1, keepdims=True) * 0.5 / rm
    xnz = (tz1 - xrm * z1 / rm) / rm * f64(gn)
    xh = xnz * sigmoid(z2) + tz2 * sigmoid(z2) * (1.0 - sigmoid(z2)) * nz
    y = xh * f64(og) + f64(base)
    Y = y.reshape(G * M, N)
    words, scales = planes(Y)
    return Y, words, scales

@@ -1,0 +1,263 @@
+from contextlib import ExitStack
+
+import concourse.mybir as mybir
+
+G, D, M, N = 2, 256, 256, 512
+FLOPS = 4 * 2 * G * D * M * N
+
+F32 = mybir.dt.float32
+BF16 = mybir.dt.bfloat16
+I32 = mybir.dt.int32
+U32 = mybir.dt.uint32
+U8 = mybir.dt.uint8
+FP8X4 = mybir.dt.float8_e4m3fn_x4
+ACT = mybir.ActivationFunctionType
+ALU = mybir.AluOpType
+
+P = 128
+PACK = 4
+ROWS = D // PACK
+HALF = N // 2
+EPS = 0.01
+TILES = [(0, 0), (1, 0), (0, 1), (1, 1)]
+X_SPLIT = 336
+PLANE_SPLIT = 160
+
+
+def interleave(copy, grouped, raw, first, last, offset=0):
+    dst = grouped[:, PACK * (first - offset) : PACK * (last - offset)]
+    copy(
+        out=dst.rearrange("p (c i t) -> p c t i", i=4, t=PACK),
+        in_=raw[:, :, first:last].rearrange("p t (c i) -> p c t i", i=4),
+    )
+
+
+def tile_rows_pl_tnrownorm_kernel(tc, x, w1, w2, gn, dx, og, base, out_0, out_1, out_2):
+    nc = tc.nc
+    with ExitStack() as ctx:
+        sb = ctx.enter_context(tc.tile_pool(name="sb", bufs=1))
+        ps = ctx.enter_context(tc.psum_pool(name="ps", bufs=1))
+        ctx.enter_context(tc.manual_schedule())
+
+        def f32_tiles(name, width):
+            return [sb.tile([P, width], F32, name="%s%d" % (name, i), align_bytes=64) for i in range(len(TILES))]
+
+        def mx_operand(name, width):
+            codes = sb.tile([P, width], U32, name=name + "_codes", align_bytes=64)
+            scales = sb.tile([P, width], U8, name=name + "_scales", align_bytes=64)
+            return codes, scales
+
+        def quantize(operand, grouped, first, last):
+            codes, scales = operand
+            nc.vector.quantize_mx(out=codes[:, first:last].bitcast(FP8X4), scales=scales[:, first:last], in_=grouped[:])
+
+        def product(bank, weights, moving, i):
+            g, h = TILES[i]
+            rows = slice(ROWS * g, ROWS * (g + 1))
+            cols = slice(P * h, P * (h + 1))
+            nc.tensor.matmul_mx(
+                out=bank[:],
+                lhsT=weights[0][rows, cols].bitcast(FP8X4),
+                lhsT_scale=weights[1][rows, cols],
+                rhs=moving[0][rows, :].bitcast(FP8X4),
+                rhs_scale=moving[1][rows, :],
+                start=True,
+                stop=True,
+            )
+
+        banks = [[ps.tile([P, N], F32, name="bank%d_%d" % (g, b)) for b in range(4)] for g in range(G)]
+        z1 = [banks[g][3 * h] for g, h in TILES]
+        z2 = [banks[g][1] for g, h in TILES]
+        tz1 = [banks[g][2 - 2 * h] for g, h in TILES]
+        tz2 = [banks[g][1 + h] for g, h in TILES]
+
+        w1_raw = sb.tile([P, PACK, M], F32, align_bytes=64)
+        w2_raw = sb.tile([P, PACK, M], F32, align_bytes=64)
+        x_raw = sb.tile([P, PACK, N], F32, align_bytes=64)
+        dx_raw = [sb.tile([P, PACK, HALF], F32, name="dx_raw%d" % c, align_bytes=64) for c in range(2)]
+        gn_sb = sb.tile([P, G, 2], F32)
+        og_sb = sb.tile([P, G, 2], F32)
+        base_sb = sb.tile([P, G * 2, N], F32, align_bytes=64)
+        split = "g (p j) n -> (g p) j n"
+        nc.sync.dma_start(out=w1_raw[:], in_=w1.rearrange(split, j=PACK))
+        nc.sync.dma_start(out=x_raw[:], in_=x.rearrange(split, j=PACK))
+        nc.sync.dma_start(out=w2_raw[:], in_=w2.rearrange(split, j=PACK))
+        for c in range(2):
+            nc.sync.dma_start(out=dx_raw[c][:], in_=dx.rearrange(split, j=PACK)[:, :, HALF * c : HALF * (c + 1)])
+        with nc.allow_non_contiguous_dma(reason="one gain a partition"):
+            nc.sync.dma_start(out=gn_sb[:], in_=gn.rearrange("g (h p) o -> p g (h o)", p=P))
+            nc.sync.dma_start(out=og_sb[:], in_=og.rearrange("g (h p) o -> p g (h o)", p=P))
+        nc.sync.dma_start(out=base_sb[:], in_=base.rearrange("g (h p) n -> p (g h) n", p=P))
+
+        gate = f32_tiles("gate", N)
+        gate_a = f32_tiles("gate_a", N)
+        z1_mean = f32_tiles("z1_mean", N)
+        slope = f32_tiles("slope", N)
+        cross = f32_tiles("cross", N)
+        inner = f32_tiles("inner", N)
+        change = f32_tiles("change", N)
+        y = f32_tiles("y", N)
+        sum_sq = sb.tile([P, 4], F32)
+        mean_sq = sb.tile([P, 4], F32)
+        inv_ms = sb.tile([P, 4], F32)
+        kappa = sb.tile([P, 4], F32)
+        inv_rm = sb.tile([P, 4], F32)
+        gains = sb.tile([P, 4], F32)
+        amp = sb.tile([P, 4], F32)
+        minus_half = sb.tile([P, 2], F32)
+
+        nc.gpsimd.memset(minus_half[:], -0.5)
+        nc.scalar.activation(out=gate[0][:, 0:1], in_=minus_half[:, 0:1], func=ACT.Sigmoid)
+
+        w1_q = mx_operand("w1", M)
+        w2_q = mx_operand("w2", M)
+        x_q = mx_operand("x", N)
+        dx_q = mx_operand("dx", N)
+        w1_bf = sb.tile([P, PACK * M], BF16, align_bytes=64)
+        w2_bf = sb.tile([P, PACK * M], BF16, align_bytes=64)
+        x_bf = [sb.tile([P, PACK * HALF], BF16, name="x_bf%d" % c, align_bytes=64) for c in range(2)]
+        dx_bf = [sb.tile([P, PACK * P], BF16, name="dx_bf%d" % c, align_bytes=64) for c in range(4)]
+
+        interleave(nc.vector.tensor_copy, w1_bf, w1_raw, 0, M)
+        quantize(w1_q, w1_bf, 0, M)
+        interleave(nc.vector.tensor_copy, x_bf[0], x_raw, 0, HALF)
+        interleave(nc.scalar.copy, x_bf[1], x_raw, X_SPLIT, N, HALF)
+        interleave(nc.vector.tensor_copy, x_bf[1], x_raw, HALF, X_SPLIT, HALF)
+        for c in range(2):
+            quantize(x_q, x_bf[c], HALF * c, HALF * (c + 1))
+        for i in range(2):
+            product(z1[i], w1_q, x_q, i)
+        interleave(nc.scalar.copy, w2_bf, w2_raw, P, M)
+        interleave(nc.vector.tensor_copy, w2_bf, w2_raw, 0, P)
+        quantize(w2_q, w2_bf, 0, M)
+        for i in range(2):
+            product(z2[i], w2_q, x_q, i)
+        for i in range(2, 4):
+            product(z1[i], w1_q, x_q, i)
+
+        def squares(pair):
+            for i in pair:
+                nc.scalar.activation(out=gate[i][:], in_=z1[i][:], func=ACT.Square, accum_out=sum_sq[:, i : i + 1])
+            cols = slice(pair[0], pair[1] + 1)
+            nc.scalar.activation(out=mean_sq[:, cols], in_=sum_sq[:, cols], func=ACT.Identity, scale=1.0 / N, bias=EPS)
+
+        def amplitudes(pair):
+            cols = slice(pair[0], pair[1] + 1)
+            nc.gpsimd.tensor_tensor(out=inv_rm[:, cols], in0=mean_sq[:, cols], in1=minus_half[:], op=ALU.pow)
+            nc.gpsimd.tensor_tensor(out=amp[:, cols], in0=inv_rm[:, cols], in1=gains[:, cols], op=ALU.mult)
+
+        def copy_and_gate(i):
+            nc.scalar.activation(out=z1_mean[i][:], in_=z1[i][:], func=ACT.Copy, scale=1.0 / N)
+            nc.scalar.activation(out=gate[i][:], in_=z2[i][:], func=ACT.Sigmoid)
+
+        squares((0, 1))
+        copy_and_gate(0)
+        for c in range(2):
+            for b in range(2):
+                interleave(nc.vector.tensor_copy, dx_bf[2 * c + b], dx_raw[c], P * b, P * (b + 1), P * b)
+            for b in range(2):
+                quantize(dx_q, dx_bf[2 * c + b], HALF * c + P * b, HALF * c + P * (b + 1))
+        nc.vector.reciprocal(out=inv_ms[:, 0:2], in_=mean_sq[:, 0:2])
+        product(tz1[0], w1_q, dx_q, 0)
+        product(tz1[1], w1_q, dx_q, 1)
+        product(tz2[0], w2_q, dx_q, 0)
+        nc.gpsimd.tensor_tensor(
+            out=gains[:].rearrange("p (h g) -> p g h", g=G), in0=gn_sb[:], in1=og_sb[:], op=ALU.mult
+        )
+        amplitudes((0, 1))
+        copy_and_gate(1)
+        product(tz2[1], w2_q, dx_q, 1)
+        for i in range(2):
+            nc.gpsimd.tensor_scalar(
+                out=gate_a[i][:], in0=gate[i][:], scalar1=amp[:, i : i + 1], scalar2=0.0, op0=ALU.mult, op1=ALU.add
+            )
+        squares((2, 3))
+        amplitudes((2, 3))
+
+        halves = [slice(0, HALF), slice(HALF, N)]
+        plane_raw = [sb.tile([P, PACK, HALF], F32, name="plane_raw%d" % h, align_bytes=64) for h in range(2)]
+        plane_bf = [sb.tile([P, PACK * HALF], BF16, name="plane_bf%d" % h, align_bytes=64) for h in range(2)]
+        plane_codes = [sb.tile([P, HALF], U32, name="plane_codes%d" % h, align_bytes=64) for h in range(2)]
+        plane_scales = sb.tile([P, HALF], U8, align_bytes=64)
+        words = out_1.rearrange("s p n u -> (s p) (n u)").bitcast(I32).rearrange("(g h q) n -> h g q n", g=G, h=2)
+        scale_rows = out_2.rearrange("s f n -> (s f) n").bitcast(I32)
+
+        def from_psum(i):
+            nc.vector.scalar_tensor_tensor(
+                out=inner[i][:], in0=tz1[i][:], scalar=inv_ms[:, i : i + 1], in1=z1_mean[i][:],
+                op0=ALU.mult, op1=ALU.mult, accum_out=kappa[:, i : i + 1],
+            )
+            for cols in halves:
+                nc.vector.scalar_tensor_tensor(
+                    out=slope[i][:, cols], in0=gate[i][:, cols], scalar=1.0, in1=tz2[i][:, cols],
+                    op0=ALU.subtract, op1=ALU.mult,
+                )
+            if i < 2:
+                product(z2[i + 2], w2_q, x_q, i + 2)
+            for cols in halves:
+                nc.vector.scalar_tensor_tensor(
+                    out=cross[i][:, cols], in0=slope[i][:, cols], scalar=kappa[:, i : i + 1], in1=z1[i][:, cols],
+                    op0=ALU.add, op1=ALU.mult,
+                )
+            if i < 2:
+                product(tz1[i + 2], w1_q, dx_q, i + 2)
+            for cols in halves:
+                nc.vector.tensor_tensor(out=inner[i][:, cols], in0=tz1[i][:, cols], in1=cross[i][:, cols], op=ALU.subtract)
+            if i < 2:
+                product(tz2[i + 2], w2_q, dx_q, i + 2)
+
+        def regroup_and_store(i):
+            g, h = TILES[i]
+            for c in range(2):
+                first = 64 * c + 32 * g
+                nc.sync.dma_start(out=plane_raw[h][first : first + 32, :, :], in_=y[i][:, halves[c]])
+            row = M * g + P * h
+            nc.sync.dma_start(out=out_0[row : row + P, :], in_=y[i][:])
+
+        def finish_on_gpsimd(i):
+            g, h = TILES[i]
+            nc.gpsimd.tensor_tensor(out=change[i][:], in0=inner[i][:], in1=gate_a[i][:], op=ALU.mult)
+            nc.gpsimd.tensor_tensor(out=y[i][:], in0=change[i][:], in1=base_sb[:, 2 * g + h, :], op=ALU.add)
+            regroup_and_store(i)
+
+        def quantize_plane(h, queues):
+            nc.vector.quantize_mx(
+                out=plane_codes[h][:].bitcast(FP8X4), scales=plane_scales[4 * h : P, :], in_=plane_bf[h][:]
+            )
+            for c in range(2):
+                queues[c].dma_start(
+                    out=words[h][:, :, halves[c]], in_=plane_codes[h][64 * c : 64 * (c + 1), :].bitcast(I32)
+                )
+
+        from_psum(0)
+        finish_on_gpsimd(0)
+        copy_and_gate(2)
+        from_psum(1)
+        nc.vector.reciprocal(out=inv_ms[:, 2:4], in_=mean_sq[:, 2:4])
+        finish_on_gpsimd(1)
+        copy_and_gate(3)
+        nc.scalar.activation(out=gate_a[2][:], in_=gate[2][:], func=ACT.Copy, scale=amp[:, 2:3])
+        from_psum(2)
+        finish_on_gpsimd(2)
+        interleave(nc.scalar.copy, plane_bf[0], plane_raw[0], 0, HALF)
+        from_psum(3)
+        for cols in halves:
+            nc.vector.scalar_tensor_tensor(
+                out=change[3][:, cols], in0=inner[3][:, cols], scalar=amp[:, 3:4], in1=gate[3][:, cols],
+                op0=ALU.mult, op1=ALU.mult,
+            )
+        for cols in halves:
+            nc.vector.tensor_tensor(out=y[3][:, cols], in0=change[3][:, cols], in1=base_sb[:, 3, cols], op=ALU.add)
+        regroup_and_store(3)
+        quantize_plane(0, [nc.scalar, nc.scalar])
+        interleave(nc.vector.tensor_copy, plane_bf[1], plane_raw[1], 0, PLANE_SPLIT)
+        interleave(nc.scalar.copy, plane_bf[1], plane_raw[1], PLANE_SPLIT, HALF)
+        quantize_plane(1, [nc.sync, nc.scalar])
+        for c in range(2):
+            for g in range(G):
+                first = 64 * c + 32 * g
+                queue = nc.sync if g == 0 else nc.scalar
+                queue.dma_start(
+                    out=scale_rows[8 * g : 8 * (g + 1), 64 * c : 64 * (c + 1)],
+                    in_=plane_scales[first : first + 8, :].bitcast(I32),
+                )

@@ -27,8 +27,8 @@ PLANE_SPLIT = 160
 def interleave(copy, grouped, raw, first, last, offset=0):
     dst = grouped[:, PACK * (first - offset) : PACK * (last - offset)]
     copy(
-        out=dst.rearrange("p (c i t) -> p c t i", i=4, t=PACK),
-        in_=raw[:, :, first:last].rearrange("p t (c i) -> p c t i", i=4),
+        out=dst.rearrange("p (c i t) -> p c t i", i=2, t=PACK),
+        in_=raw[:, :, first:last].rearrange("p t (c i) -> p c t i", i=2),
     )
 
 
@@ -75,8 +75,9 @@ def tile_rows_pl_tnrownorm_kernel(tc, x, w1, w2, gn, dx, og, base, out_0, out_1,
         w2_raw = sb.tile([P, PACK, M], F32, align_bytes=64)
         x_raw = sb.tile([P, PACK, N], F32, align_bytes=64)
         dx_raw = [sb.tile([P, PACK, HALF], F32, name="dx_raw%d" % c, align_bytes=64) for c in range(2)]
-        gn_sb = sb.tile([P, G, 2], F32)
-        og_sb = sb.tile([P, G, 2], F32)
+        gain_rows = sb.tile([P, 32], F32, align_bytes=64)
+        gain_cols = sb.tile([P, 32], F32, align_bytes=64)
+        nc.vector.memset(gain_rows[:], 0.0)
         base_sb = sb.tile([P, G * 2, N], F32, align_bytes=64)
         split = "g (p j) n -> (g p) j n"
         nc.sync.dma_start(out=w1_raw[:], in_=w1.rearrange(split, j=PACK))
@@ -84,9 +85,8 @@ def tile_rows_pl_tnrownorm_kernel(tc, x, w1, w2, gn, dx, og, base, out_0, out_1,
         nc.sync.dma_start(out=w2_raw[:], in_=w2.rearrange(split, j=PACK))
         for c in range(2):
             nc.sync.dma_start(out=dx_raw[c][:], in_=dx.rearrange(split, j=PACK)[:, :, HALF * c : HALF * (c + 1)])
-        with nc.allow_non_contiguous_dma(reason="one gain a partition"):
-            nc.sync.dma_start(out=gn_sb[:], in_=gn.rearrange("g (h p) o -> p g (h o)", p=P))
-            nc.sync.dma_start(out=og_sb[:], in_=og.rearrange("g (h p) o -> p g (h o)", p=P))
+        for e, gain in enumerate((gn, og)):
+            nc.sync.dma_start(out=gain_rows[e:P:8, :], in_=gain.rearrange("g (h q r) o -> q (g h) (r o)", h=2, q=4))
         nc.sync.dma_start(out=base_sb[:], in_=base.rearrange("g (h p) n -> p (g h) n", p=P))
 
         gate = f32_tiles("gate", N)
@@ -161,18 +161,20 @@ def tile_rows_pl_tnrownorm_kernel(tc, x, w1, w2, gn, dx, og, base, out_0, out_1,
         product(tz1[0], w1_q, dx_q, 0)
         product(tz1[1], w1_q, dx_q, 1)
         product(tz2[0], w2_q, dx_q, 0)
+        nc.vector.transpose(out=gain_cols[:], in_=gain_rows[:])
+        by_tile = gain_cols[:].rearrange("p (g h e) -> p h g e", g=G, h=2)
         nc.gpsimd.tensor_tensor(
-            out=gains[:].rearrange("p (h g) -> p g h", g=G), in0=gn_sb[:], in1=og_sb[:], op=ALU.mult
+            out=gains[:].rearrange("p (h g) -> p h g", g=G), in0=by_tile[:, :, :, 0], in1=by_tile[:, :, :, 1], op=ALU.mult
         )
         amplitudes((0, 1))
-        copy_and_gate(1)
-        product(tz2[1], w2_q, dx_q, 1)
-        for i in range(2):
-            nc.gpsimd.tensor_scalar(
-                out=gate_a[i][:], in0=gate[i][:], scalar1=amp[:, i : i + 1], scalar2=0.0, op0=ALU.mult, op1=ALU.add
-            )
+        nc.gpsimd.tensor_scalar(
+            out=gate_a[0][:], in0=gate[0][:], scalar1=amp[:, 0:1], scalar2=0.0, op0=ALU.mult, op1=ALU.add
+        )
         squares((2, 3))
         amplitudes((2, 3))
+        copy_and_gate(1)
+        product(tz2[1], w2_q, dx_q, 1)
+        nc.scalar.activation(out=gate_a[1][:], in_=gate[1][:], func=ACT.Copy, scale=amp[:, 1:2])
 
         halves = [slice(0, HALF), slice(HALF, N)]
         plane_raw = [sb.tile([P, PACK, HALF], F32, name="plane_raw%d" % h, align_bytes=64) for h in range(2)]
@@ -184,7 +186,7 @@ def tile_rows_pl_tnrownorm_kernel(tc, x, w1, w2, gn, dx, og, base, out_0, out_1,
 
         def from_psum(i):
             nc.vector.scalar_tensor_tensor(
-                out=inner[i][:], in0=tz1[i][:], scalar=inv_ms[:, i : i + 1], in1=z1_mean[i][:],
+                out=inner[i][:], in0=z1_mean[i][:], scalar=inv_ms[:, i : i + 1], in1=tz1[i][:],
                 op0=ALU.mult, op1=ALU.mult, accum_out=kappa[:, i : i + 1],
             )
             for cols in halves:
@@ -202,23 +204,25 @@ def tile_rows_pl_tnrownorm_kernel(tc, x, w1, w2, gn, dx, og, base, out_0, out_1,
             if i < 2:
                 product(tz1[i + 2], w1_q, dx_q, i + 2)
             for cols in halves:
-                nc.vector.tensor_tensor(out=inner[i][:, cols], in0=tz1[i][:, cols], in1=cross[i][:, cols], op=ALU.subtract)
+                nc.vector.tensor_tensor(out=inner[i][:, cols], in0=cross[i][:, cols], in1=tz1[i][:, cols], op=ALU.subtract)
             if i < 2:
                 product(tz2[i + 2], w2_q, dx_q, i + 2)
 
-        def regroup_and_store(i):
+        def regroup(i, queues):
             g, h = TILES[i]
             for c in range(2):
                 first = 64 * c + 32 * g
-                nc.sync.dma_start(out=plane_raw[h][first : first + 32, :, :], in_=y[i][:, halves[c]])
+                queues[c].dma_start(out=plane_raw[h][first : first + 32, :, :], in_=y[i][:, halves[c]])
+
+        def store(i):
+            g, h = TILES[i]
             row = M * g + P * h
             nc.sync.dma_start(out=out_0[row : row + P, :], in_=y[i][:])
 
         def finish_on_gpsimd(i):
             g, h = TILES[i]
             nc.gpsimd.tensor_tensor(out=change[i][:], in0=inner[i][:], in1=gate_a[i][:], op=ALU.mult)
-            nc.gpsimd.tensor_tensor(out=y[i][:], in0=change[i][:], in1=base_sb[:, 2 * g + h, :], op=ALU.add)
-            regroup_and_store(i)
+            nc.gpsimd.tensor_tensor(out=y[i][:], in0=base_sb[:, 2 * g + h, :], in1=change[i][:], op=ALU.subtract)
 
         def quantize_plane(h, queues):
             nc.vector.quantize_mx(
@@ -231,15 +235,20 @@ def tile_rows_pl_tnrownorm_kernel(tc, x, w1, w2, gn, dx, og, base, out_0, out_1,
 
         from_psum(0)
         finish_on_gpsimd(0)
+        regroup(0, [nc.sync, nc.sync])
+        store(0)
         copy_and_gate(2)
         from_psum(1)
         nc.vector.reciprocal(out=inv_ms[:, 2:4], in_=mean_sq[:, 2:4])
         finish_on_gpsimd(1)
+        regroup(1, [nc.sync, nc.sync])
+        store(1)
         copy_and_gate(3)
         nc.scalar.activation(out=gate_a[2][:], in_=gate[2][:], func=ACT.Copy, scale=amp[:, 2:3])
         from_psum(2)
         finish_on_gpsimd(2)
         interleave(nc.scalar.copy, plane_bf[0], plane_raw[0], 0, HALF)
+        regroup(2, [nc.sync, nc.scalar])
         from_psum(3)
         for cols in halves:
             nc.vector.scalar_tensor_tensor(
@@ -247,8 +256,10 @@ def tile_rows_pl_tnrownorm_kernel(tc, x, w1, w2, gn, dx, og, base, out_0, out_1,
                 op0=ALU.mult, op1=ALU.mult,
             )
         for cols in halves:
-            nc.vector.tensor_tensor(out=y[3][:, cols], in0=change[3][:, cols], in1=base_sb[:, 3, cols], op=ALU.add)
-        regroup_and_store(3)
+            nc.vector.tensor_tensor(out=y[3][:, cols], in0=base_sb[:, 3, cols], in1=change[3][:, cols], op=ALU.subtract)
+        regroup(3, [nc.sync, nc.scalar])
+        store(2)
+        store(3)
         quantize_plane(0, [nc.scalar, nc.scalar])
         interleave(nc.vector.tensor_copy, plane_bf[1], plane_raw[1], 0, PLANE_SPLIT)
         interleave(nc.scalar.copy, plane_bf[1], plane_raw[1], PLANE_SPLIT, HALF)

@@ -66,10 +66,10 @@ def tile_rows_pl_tnrownorm_kernel(tc, x, w1, w2, gn, dx, og, base, out_0, out_1,
             )
 
         banks = [[ps.tile([P, N], F32, name="bank%d_%d" % (g, b)) for b in range(4)] for g in range(G)]
-        z1 = [banks[g][3 * h] for g, h in TILES]
-        z2 = [banks[g][1] for g, h in TILES]
+        z1 = [banks[g][h] for g, h in TILES]
+        z2 = [banks[g][1 + 2 * h] for g, h in TILES]
         tz1 = [banks[g][2 - 2 * h] for g, h in TILES]
-        tz2 = [banks[g][1 + h] for g, h in TILES]
+        tz2 = [banks[g][3 - h] for g, h in TILES]
 
         w1_raw = sb.tile([P, PACK, M], F32, align_bytes=64)
         w2_raw = sb.tile([P, PACK, M], F32, align_bytes=64)
@@ -80,17 +80,16 @@ def tile_rows_pl_tnrownorm_kernel(tc, x, w1, w2, gn, dx, og, base, out_0, out_1,
         nc.vector.memset(gain_rows[:], 0.0)
         base_sb = sb.tile([P, G * 2, N], F32, align_bytes=64)
         split = "g (p j) n -> (g p) j n"
-        nc.sync.dma_start(out=w1_raw[:], in_=w1.rearrange(split, j=PACK))
         nc.sync.dma_start(out=x_raw[:], in_=x.rearrange(split, j=PACK))
-        nc.sync.dma_start(out=w2_raw[:], in_=w2.rearrange(split, j=PACK))
+        nc.sync.dma_start(out=w1_raw[:], in_=w1.rearrange(split, j=PACK))
         for c in range(2):
             nc.sync.dma_start(out=dx_raw[c][:], in_=dx.rearrange(split, j=PACK)[:, :, HALF * c : HALF * (c + 1)])
+        nc.sync.dma_start(out=w2_raw[:], in_=w2.rearrange(split, j=PACK))
         for e, gain in enumerate((gn, og)):
             nc.sync.dma_start(out=gain_rows[e:P:8, :], in_=gain.rearrange("g (h q r) o -> q (g h) (r o)", h=2, q=4))
         nc.sync.dma_start(out=base_sb[:], in_=base.rearrange("g (h p) n -> p (g h) n", p=P))
 
         gate = f32_tiles("gate", N)
-        gate_a = f32_tiles("gate_a", N)
         z1_mean = f32_tiles("z1_mean", N)
         slope = f32_tiles("slope", N)
         cross = f32_tiles("cross", N)
@@ -113,68 +112,62 @@ def tile_rows_pl_tnrownorm_kernel(tc, x, w1, w2, gn, dx, og, base, out_0, out_1,
         w2_q = mx_operand("w2", M)
         x_q = mx_operand("x", N)
         dx_q = mx_operand("dx", N)
-        w1_bf = sb.tile([P, PACK * M], BF16, align_bytes=64)
-        w2_bf = sb.tile([P, PACK * M], BF16, align_bytes=64)
+        w1_bf = [sb.tile([P, PACK * P], BF16, name="w1_bf%d" % h, align_bytes=64) for h in range(2)]
+        w2_bf = [sb.tile([P, PACK * P], BF16, name="w2_bf%d" % h, align_bytes=64) for h in range(2)]
         x_bf = [sb.tile([P, PACK * HALF], BF16, name="x_bf%d" % c, align_bytes=64) for c in range(2)]
         dx_bf = [sb.tile([P, PACK * P], BF16, name="dx_bf%d" % c, align_bytes=64) for c in range(4)]
 
-        interleave(nc.vector.tensor_copy, w1_bf, w1_raw, 0, M)
-        quantize(w1_q, w1_bf, 0, M)
         interleave(nc.vector.tensor_copy, x_bf[0], x_raw, 0, HALF)
         interleave(nc.scalar.copy, x_bf[1], x_raw, X_SPLIT, N, HALF)
         interleave(nc.vector.tensor_copy, x_bf[1], x_raw, HALF, X_SPLIT, HALF)
         for c in range(2):
             quantize(x_q, x_bf[c], HALF * c, HALF * (c + 1))
+        interleave(nc.scalar.copy, w1_bf[0], w1_raw, 0, P)
+        interleave(nc.vector.tensor_copy, w1_bf[1], w1_raw, P, M, P)
+        for h in range(2):
+            quantize(w1_q, w1_bf[h], P * h, P * (h + 1))
         for i in range(2):
-            product(z1[i], w1_q, x_q, i)
-        interleave(nc.scalar.copy, w2_bf, w2_raw, P, M)
-        interleave(nc.vector.tensor_copy, w2_bf, w2_raw, 0, P)
-        quantize(w2_q, w2_bf, 0, M)
-        for i in range(2):
-            product(z2[i], w2_q, x_q, i)
-        for i in range(2, 4):
             product(z1[i], w1_q, x_q, i)
 
-        def squares(pair):
-            for i in pair:
-                nc.scalar.activation(out=gate[i][:], in_=z1[i][:], func=ACT.Square, accum_out=sum_sq[:, i : i + 1])
-            cols = slice(pair[0], pair[1] + 1)
-            nc.scalar.activation(out=mean_sq[:, cols], in_=sum_sq[:, cols], func=ACT.Identity, scale=1.0 / N, bias=EPS)
+        def row_stats(i):
+            col = slice(i, i + 1)
+            nc.scalar.activation(out=gate[i][:], in_=z1[i][:], func=ACT.Square, accum_out=sum_sq[:, col])
+            nc.scalar.activation(out=z1_mean[i][:], in_=z1[i][:], func=ACT.Copy, scale=1.0 / N)
+            nc.scalar.activation(out=mean_sq[:, col], in_=sum_sq[:, col], func=ACT.Identity, scale=1.0 / N, bias=EPS)
 
         def amplitudes(pair):
             cols = slice(pair[0], pair[1] + 1)
             nc.gpsimd.tensor_tensor(out=inv_rm[:, cols], in0=mean_sq[:, cols], in1=minus_half[:], op=ALU.pow)
             nc.gpsimd.tensor_tensor(out=amp[:, cols], in0=inv_rm[:, cols], in1=gains[:, cols], op=ALU.mult)
 
-        def copy_and_gate(i):
-            nc.scalar.activation(out=z1_mean[i][:], in_=z1[i][:], func=ACT.Copy, scale=1.0 / N)
+        def sigmoid(i):
             nc.scalar.activation(out=gate[i][:], in_=z2[i][:], func=ACT.Sigmoid)
 
-        squares((0, 1))
-        copy_and_gate(0)
-        for c in range(2):
-            for b in range(2):
-                interleave(nc.vector.tensor_copy, dx_bf[2 * c + b], dx_raw[c], P * b, P * (b + 1), P * b)
-            for b in range(2):
-                quantize(dx_q, dx_bf[2 * c + b], HALF * c + P * b, HALF * c + P * (b + 1))
-        nc.vector.reciprocal(out=inv_ms[:, 0:2], in_=mean_sq[:, 0:2])
-        product(tz1[0], w1_q, dx_q, 0)
-        product(tz1[1], w1_q, dx_q, 1)
-        product(tz2[0], w2_q, dx_q, 0)
-        nc.vector.transpose(out=gain_cols[:], in_=gain_rows[:])
-        by_tile = gain_cols[:].rearrange("p (g h e) -> p h g e", g=G, h=2)
-        nc.gpsimd.tensor_tensor(
-            out=gains[:].rearrange("p (h g) -> p h g", g=G), in0=by_tile[:, :, :, 0], in1=by_tile[:, :, :, 1], op=ALU.mult
-        )
-        amplitudes((0, 1))
-        nc.gpsimd.tensor_scalar(
-            out=gate_a[0][:], in0=gate[0][:], scalar1=amp[:, 0:1], scalar2=0.0, op0=ALU.mult, op1=ALU.add
-        )
-        squares((2, 3))
-        amplitudes((2, 3))
-        copy_and_gate(1)
-        product(tz2[1], w2_q, dx_q, 1)
-        nc.scalar.activation(out=gate_a[1][:], in_=gate[1][:], func=ACT.Copy, scale=amp[:, 1:2])
+        def inverse(i):
+            nc.vector.reciprocal(out=inv_ms[:, i : i + 1], in_=mean_sq[:, i : i + 1])
+
+        interleave(nc.scalar.copy, dx_bf[1], dx_raw[0], P, HALF, P)
+        interleave(nc.vector.tensor_copy, dx_bf[0], dx_raw[0], 0, P)
+        for b in range(2):
+            quantize(dx_q, dx_bf[b], P * b, P * (b + 1))
+        row_stats(0)
+        for b in range(2):
+            interleave(nc.vector.tensor_copy, dx_bf[2 + b], dx_raw[1], P * b, P * (b + 1), P * b)
+        for b in range(2, 4):
+            quantize(dx_q, dx_bf[b], P * b, P * (b + 1))
+        for i in range(2):
+            product(tz1[i], w1_q, dx_q, i)
+        interleave(nc.vector.tensor_copy, w2_bf[0], w2_raw, 0, P)
+        inverse(0)
+        quantize(w2_q, w2_bf[0], 0, P)
+        for i in range(2):
+            product(z2[i], w2_q, x_q, i)
+            product(tz2[i], w2_q, dx_q, i)
+        row_stats(1)
+        for i in range(2):
+            sigmoid(i)
+            product(z1[i + 2], w1_q, x_q, i + 2)
+        interleave(nc.scalar.copy, w2_bf[1], w2_raw, P, M, P)
 
         halves = [slice(0, HALF), slice(HALF, N)]
         plane_raw = [sb.tile([P, PACK, HALF], F32, name="plane_raw%d" % h, align_bytes=64) for h in range(2)]
@@ -184,29 +177,38 @@ def tile_rows_pl_tnrownorm_kernel(tc, x, w1, w2, gn, dx, og, base, out_0, out_1,
         words = out_1.rearrange("s p n u -> (s p) (n u)").bitcast(I32).rearrange("(g h q) n -> h g q n", g=G, h=2)
         scale_rows = out_2.rearrange("s f n -> (s f) n").bitcast(I32)
 
-        def from_psum(i):
+        every = slice(0, N)
+
+        def step_kappa(i):
             nc.vector.scalar_tensor_tensor(
                 out=inner[i][:], in0=z1_mean[i][:], scalar=inv_ms[:, i : i + 1], in1=tz1[i][:],
                 op0=ALU.mult, op1=ALU.mult, accum_out=kappa[:, i : i + 1],
             )
-            for cols in halves:
-                nc.vector.scalar_tensor_tensor(
-                    out=slope[i][:, cols], in0=gate[i][:, cols], scalar=1.0, in1=tz2[i][:, cols],
-                    op0=ALU.subtract, op1=ALU.mult,
-                )
-            if i < 2:
-                product(z2[i + 2], w2_q, x_q, i + 2)
-            for cols in halves:
-                nc.vector.scalar_tensor_tensor(
-                    out=cross[i][:, cols], in0=slope[i][:, cols], scalar=kappa[:, i : i + 1], in1=z1[i][:, cols],
-                    op0=ALU.add, op1=ALU.mult,
-                )
-            if i < 2:
-                product(tz1[i + 2], w1_q, dx_q, i + 2)
-            for cols in halves:
-                nc.vector.tensor_tensor(out=inner[i][:, cols], in0=cross[i][:, cols], in1=tz1[i][:, cols], op=ALU.subtract)
+
+        def step_slope(i):
+            nc.vector.scalar_tensor_tensor(
+                out=slope[i][:], in0=gate[i][:], scalar=1.0, in1=tz2[i][:], op0=ALU.subtract, op1=ALU.mult
+            )
+
+        def step_cross(i):
+            nc.vector.scalar_tensor_tensor(
+                out=cross[i][:], in0=slope[i][:], scalar=kappa[:, i : i + 1], in1=z1[i][:], op0=ALU.add, op1=ALU.mult
+            )
+
+        def step_inner(i):
+            nc.vector.tensor_tensor(out=inner[i][:], in0=cross[i][:], in1=tz1[i][:], op=ALU.subtract)
             if i < 2:
                 product(tz2[i + 2], w2_q, dx_q, i + 2)
+
+        def step_change(i, cols=every):
+            nc.vector.scalar_tensor_tensor(
+                out=change[i][:, cols], in0=inner[i][:, cols], scalar=amp[:, i : i + 1], in1=gate[i][:, cols],
+                op0=ALU.mult, op1=ALU.mult,
+            )
+
+        def step_y(i, cols=every):
+            g, h = TILES[i]
+            nc.vector.tensor_tensor(out=y[i][:, cols], in0=base_sb[:, 2 * g + h, cols], in1=change[i][:, cols], op=ALU.subtract)
 
         def regroup(i, queues):
             g, h = TILES[i]
@@ -219,11 +221,6 @@ def tile_rows_pl_tnrownorm_kernel(tc, x, w1, w2, gn, dx, og, base, out_0, out_1,
             row = M * g + P * h
             nc.sync.dma_start(out=out_0[row : row + P, :], in_=y[i][:])
 
-        def finish_on_gpsimd(i):
-            g, h = TILES[i]
-            nc.gpsimd.tensor_tensor(out=change[i][:], in0=inner[i][:], in1=gate_a[i][:], op=ALU.mult)
-            nc.gpsimd.tensor_tensor(out=y[i][:], in0=base_sb[:, 2 * g + h, :], in1=change[i][:], op=ALU.subtract)
-
         def quantize_plane(h, queues):
             nc.vector.quantize_mx(
                 out=plane_codes[h][:].bitcast(FP8X4), scales=plane_scales[4 * h : P, :], in_=plane_bf[h][:]
@@ -233,30 +230,55 @@ def tile_rows_pl_tnrownorm_kernel(tc, x, w1, w2, gn, dx, og, base, out_0, out_1,
                     out=words[h][:, :, halves[c]], in_=plane_codes[h][64 * c : 64 * (c + 1), :].bitcast(I32)
                 )
 
-        from_psum(0)
-        finish_on_gpsimd(0)
+        step_kappa(0)
+        inverse(1)
+        nc.vector.transpose(out=gain_cols[:], in_=gain_rows[:])
+        by_tile = gain_cols[:].rearrange("p (g h e) -> p h g e", g=G, h=2)
+        nc.gpsimd.tensor_tensor(
+            out=gains[:].rearrange("p (h g) -> p h g", g=G), in0=by_tile[:, :, :, 0], in1=by_tile[:, :, :, 1], op=ALU.mult
+        )
+        amplitudes((0, 1))
+        step_kappa(1)
+        step_slope(0)
+        step_slope(1)
+        step_cross(0)
+        quantize(w2_q, w2_bf[1], P, M)
+        step_cross(1)
+        for i in range(2, 4):
+            product(z2[i], w2_q, x_q, i)
+            product(tz1[i], w1_q, dx_q, i)
+        row_stats(2)
+        row_stats(3)
+        amplitudes((2, 3))
+        sigmoid(2)
+        sigmoid(3)
+        for step in (step_inner, step_change):
+            step(0)
+            step(1)
+        step_y(0)
         regroup(0, [nc.sync, nc.sync])
         store(0)
-        copy_and_gate(2)
-        from_psum(1)
-        nc.vector.reciprocal(out=inv_ms[:, 2:4], in_=mean_sq[:, 2:4])
-        finish_on_gpsimd(1)
+        inverse(2)
+        step_y(1)
         regroup(1, [nc.sync, nc.sync])
         store(1)
-        copy_and_gate(3)
-        nc.scalar.activation(out=gate_a[2][:], in_=gate[2][:], func=ACT.Copy, scale=amp[:, 2:3])
-        from_psum(2)
-        finish_on_gpsimd(2)
+        inverse(3)
+        step_kappa(2)
+        step_slope(2)
+        step_kappa(3)
+        step_cross(2)
+        step_slope(3)
+        step_inner(2)
+        step_cross(3)
+        step_change(2)
+        step_inner(3)
+        step_y(2)
         interleave(nc.scalar.copy, plane_bf[0], plane_raw[0], 0, HALF)
         regroup(2, [nc.sync, nc.scalar])
-        from_psum(3)
         for cols in halves:
-            nc.vector.scalar_tensor_tensor(
-                out=change[3][:, cols], in0=inner[3][:, cols], scalar=amp[:, 3:4], in1=gate[3][:, cols],
-                op0=ALU.mult, op1=ALU.mult,
-            )
+            step_change(3, cols)
         for cols in halves:
-            nc.vector.tensor_tensor(out=y[3][:, cols], in0=base_sb[:, 3, cols], in1=change[3][:, cols], op=ALU.subtract)
+            step_y(3, cols)
         regroup(3, [nc.sync, nc.scalar])
         store(2)
         store(3)

@@ -17,18 +17,20 @@ ALU = mybir.AluOpType
 P = 128
 PACK = 4
 ROWS = D // PACK
+QUADRANT = 32
 HALF = N // 2
 EPS = 0.01
 TILES = [(0, 0), (1, 0), (0, 1), (1, 1)]
 X_SPLIT = 336
-PLANE_SPLIT = 160
+SET_SPLIT = 160
 
 
-def interleave(copy, grouped, raw, first, last, offset=0):
-    dst = grouped[:, PACK * (first - offset) : PACK * (last - offset)]
+def interleave(copy, grouped, raw, first, last, origin=0):
+    run = 2 if raw.dtype == F32 else 4
+    target = grouped[:, PACK * (first - origin) : PACK * (last - origin)]
     copy(
-        out=dst.rearrange("p (c i t) -> p c t i", i=2, t=PACK),
-        in_=raw[:, :, first:last].rearrange("p t (c i) -> p c t i", i=2),
+        out=target.rearrange("p (c i t) -> p c t i", i=run, t=PACK),
+        in_=raw[:, :, first:last].rearrange("p t (c i) -> p c t i", i=run),
     )
 
 
@@ -39,8 +41,8 @@ def tile_rows_pl_tnrownorm_kernel(tc, x, w1, w2, gn, dx, og, base, out_0, out_1,
         ps = ctx.enter_context(tc.psum_pool(name="ps", bufs=1))
         ctx.enter_context(tc.manual_schedule())
 
-        def f32_tiles(name, width):
-            return [sb.tile([P, width], F32, name="%s%d" % (name, i), align_bytes=64) for i in range(len(TILES))]
+        def tiles(name, count, shape, dtype):
+            return [sb.tile(shape, dtype, name="%s%d" % (name, i), align_bytes=64) for i in range(count)]
 
         def mx_operand(name, width):
             codes = sb.tile([P, width], U32, name=name + "_codes", align_bytes=64)
@@ -51,14 +53,14 @@ def tile_rows_pl_tnrownorm_kernel(tc, x, w1, w2, gn, dx, og, base, out_0, out_1,
             codes, scales = operand
             nc.vector.quantize_mx(out=codes[:, first:last].bitcast(FP8X4), scales=scales[:, first:last], in_=grouped[:])
 
-        def product(bank, weights, moving, i):
+        def product(banks_by_tile, weights, moving, i):
             g, h = TILES[i]
             rows = slice(ROWS * g, ROWS * (g + 1))
-            cols = slice(P * h, P * (h + 1))
+            features = slice(P * h, P * (h + 1))
             nc.tensor.matmul_mx(
-                out=bank[:],
-                lhsT=weights[0][rows, cols].bitcast(FP8X4),
-                lhsT_scale=weights[1][rows, cols],
+                out=banks_by_tile[i][:],
+                lhsT=weights[0][rows, features].bitcast(FP8X4),
+                lhsT_scale=weights[1][rows, features],
                 rhs=moving[0][rows, :].bitcast(FP8X4),
                 rhs_scale=moving[1][rows, :],
                 start=True,
@@ -66,56 +68,74 @@ def tile_rows_pl_tnrownorm_kernel(tc, x, w1, w2, gn, dx, og, base, out_0, out_1,
             )
 
         banks = [[ps.tile([P, N], F32, name="bank%d_%d" % (g, b)) for b in range(4)] for g in range(G)]
-        z1 = [banks[g][h] for g, h in TILES]
-        z2 = [banks[g][1 + 2 * h] for g, h in TILES]
-        tz1 = [banks[g][2 - 2 * h] for g, h in TILES]
-        tz2 = [banks[g][3 - h] for g, h in TILES]
+        z1 = [banks[g][(0, 1)[h]] for g, h in TILES]
+        z2 = [banks[g][(1, 3)[h]] for g, h in TILES]
+        tz1 = [banks[g][(2, 0)[h]] for g, h in TILES]
+        tz2 = [banks[g][(3, 2)[h]] for g, h in TILES]
 
         w1_raw = sb.tile([P, PACK, M], F32, align_bytes=64)
         w2_raw = sb.tile([P, PACK, M], F32, align_bytes=64)
         x_raw = sb.tile([P, PACK, N], F32, align_bytes=64)
-        dx_raw = [sb.tile([P, PACK, HALF], F32, name="dx_raw%d" % c, align_bytes=64) for c in range(2)]
-        gain_rows = sb.tile([P, 32], F32, align_bytes=64)
-        gain_cols = sb.tile([P, 32], F32, align_bytes=64)
+        dx_raw = tiles("dx_raw", 2, [P, PACK, HALF], F32)
+        gain_rows = sb.tile([P, QUADRANT], F32, align_bytes=64)
+        gain_cols = sb.tile([P, QUADRANT], F32, align_bytes=64)
+        base_sb = sb.tile([P, len(TILES), N], F32, align_bytes=64)
+        halves = [slice(0, HALF), slice(HALF, N)]
+        every = slice(0, N)
+        packed_rows = "g (p j) n -> (g p) j n"
         nc.vector.memset(gain_rows[:], 0.0)
-        base_sb = sb.tile([P, G * 2, N], F32, align_bytes=64)
-        split = "g (p j) n -> (g p) j n"
-        nc.sync.dma_start(out=x_raw[:], in_=x.rearrange(split, j=PACK))
-        nc.sync.dma_start(out=w1_raw[:], in_=w1.rearrange(split, j=PACK))
+        nc.sync.dma_start(out=x_raw[:], in_=x.rearrange(packed_rows, j=PACK))
+        nc.sync.dma_start(out=w1_raw[:], in_=w1.rearrange(packed_rows, j=PACK))
         for c in range(2):
-            nc.sync.dma_start(out=dx_raw[c][:], in_=dx.rearrange(split, j=PACK)[:, :, HALF * c : HALF * (c + 1)])
-        nc.sync.dma_start(out=w2_raw[:], in_=w2.rearrange(split, j=PACK))
+            nc.sync.dma_start(out=dx_raw[c][:], in_=dx.rearrange(packed_rows, j=PACK)[:, :, halves[c]])
+        nc.sync.dma_start(out=w2_raw[:], in_=w2.rearrange(packed_rows, j=PACK))
         for e, gain in enumerate((gn, og)):
             nc.sync.dma_start(out=gain_rows[e:P:8, :], in_=gain.rearrange("g (h q r) o -> q (g h) (r o)", h=2, q=4))
         nc.sync.dma_start(out=base_sb[:], in_=base.rearrange("g (h p) n -> p (g h) n", p=P))
 
-        gate = f32_tiles("gate", N)
-        z1_mean = f32_tiles("z1_mean", N)
-        slope = f32_tiles("slope", N)
-        cross = f32_tiles("cross", N)
-        inner = f32_tiles("inner", N)
-        change = f32_tiles("change", N)
-        y = f32_tiles("y", N)
-        sum_sq = sb.tile([P, 4], F32)
-        mean_sq = sb.tile([P, 4], F32)
-        inv_ms = sb.tile([P, 4], F32)
-        kappa = sb.tile([P, 4], F32)
-        inv_rm = sb.tile([P, 4], F32)
-        gains = sb.tile([P, 4], F32)
-        amp = sb.tile([P, 4], F32)
+        th = tiles("th", len(TILES), [P, N], F32)
+        gate_amp = tiles("gate_amp", 2, [P, N], F32)
+        z1_scaled = tiles("z1_scaled", len(TILES), [P, N], F32)
+        slope = tiles("slope", len(TILES), [P, N], F32)
+        cross = tiles("cross", len(TILES), [P, N], F32)
+        inner = tiles("inner", len(TILES), [P, N], F32)
+        change = tiles("change", len(TILES), [P, N], F32)
+        y = tiles("y", len(TILES), [P, N], F32)
+        y_bf = tiles("y_bf", 2, [P, N], BF16)
+        sum_sq = sb.tile([P, len(TILES)], F32)
+        four_ms = sb.tile([P, len(TILES)], F32)
+        inv_four_ms = sb.tile([P, len(TILES)], F32)
+        two_kappa = sb.tile([P, len(TILES)], F32)
+        inv_two_rm = sb.tile([P, len(TILES)], F32)
+        gains = sb.tile([P, len(TILES)], F32)
+        amp = tiles("amp", 2, [P, 2], F32)
         minus_half = sb.tile([P, 2], F32)
-
         nc.gpsimd.memset(minus_half[:], -0.5)
-        nc.scalar.activation(out=gate[0][:, 0:1], in_=minus_half[:, 0:1], func=ACT.Sigmoid)
+
+        def row_stats(i):
+            col = slice(i, i + 1)
+            nc.scalar.activation(out=th[i][:], in_=z1[i][:], func=ACT.Square, accum_out=sum_sq[:, col])
+            nc.scalar.activation(out=z1_scaled[i][:], in_=z1[i][:], func=ACT.Copy, scale=8.0 / N)
+            nc.scalar.activation(out=four_ms[:, col], in_=sum_sq[:, col], func=ACT.Identity, scale=4.0 / N, bias=4.0 * EPS)
+
+        def half_tanh(i):
+            nc.scalar.activation(out=th[i][:], in_=z2[i][:], func=ACT.Tanh, scale=0.5)
+
+        def inverse(i):
+            nc.vector.reciprocal(out=inv_four_ms[:, i : i + 1], in_=four_ms[:, i : i + 1])
+
+        def inverse_roots(h):
+            cols = slice(G * h, G * (h + 1))
+            nc.gpsimd.tensor_tensor(out=inv_two_rm[:, cols], in0=four_ms[:, cols], in1=minus_half[:], op=ALU.pow)
 
         w1_q = mx_operand("w1", M)
         w2_q = mx_operand("w2", M)
         x_q = mx_operand("x", N)
         dx_q = mx_operand("dx", N)
-        w1_bf = [sb.tile([P, PACK * P], BF16, name="w1_bf%d" % h, align_bytes=64) for h in range(2)]
-        w2_bf = [sb.tile([P, PACK * P], BF16, name="w2_bf%d" % h, align_bytes=64) for h in range(2)]
-        x_bf = [sb.tile([P, PACK * HALF], BF16, name="x_bf%d" % c, align_bytes=64) for c in range(2)]
-        dx_bf = [sb.tile([P, PACK * P], BF16, name="dx_bf%d" % c, align_bytes=64) for c in range(4)]
+        w1_bf = tiles("w1_bf", 2, [P, PACK * P], BF16)
+        w2_bf = tiles("w2_bf", 2, [P, PACK * P], BF16)
+        x_bf = tiles("x_bf", 2, [P, PACK * HALF], BF16)
+        dx_bf = tiles("dx_bf", 4, [P, PACK * P], BF16)
 
         interleave(nc.vector.tensor_copy, x_bf[0], x_raw, 0, HALF)
         interleave(nc.scalar.copy, x_bf[1], x_raw, X_SPLIT, N, HALF)
@@ -127,24 +147,7 @@ def tile_rows_pl_tnrownorm_kernel(tc, x, w1, w2, gn, dx, og, base, out_0, out_1,
         for h in range(2):
             quantize(w1_q, w1_bf[h], P * h, P * (h + 1))
         for i in range(2):
-            product(z1[i], w1_q, x_q, i)
-
-        def row_stats(i):
-            col = slice(i, i + 1)
-            nc.scalar.activation(out=gate[i][:], in_=z1[i][:], func=ACT.Square, accum_out=sum_sq[:, col])
-            nc.scalar.activation(out=z1_mean[i][:], in_=z1[i][:], func=ACT.Copy, scale=1.0 / N)
-            nc.scalar.activation(out=mean_sq[:, col], in_=sum_sq[:, col], func=ACT.Identity, scale=1.0 / N, bias=EPS)
-
-        def amplitudes(pair):
-            cols = slice(pair[0], pair[1] + 1)
-            nc.gpsimd.tensor_tensor(out=inv_rm[:, cols], in0=mean_sq[:, cols], in1=minus_half[:], op=ALU.pow)
-            nc.gpsimd.tensor_tensor(out=amp[:, cols], in0=inv_rm[:, cols], in1=gains[:, cols], op=ALU.mult)
-
-        def sigmoid(i):
-            nc.scalar.activation(out=gate[i][:], in_=z2[i][:], func=ACT.Sigmoid)
-
-        def inverse(i):
-            nc.vector.reciprocal(out=inv_ms[:, i : i + 1], in_=mean_sq[:, i : i + 1])
+            product(z1, w1_q, x_q, i)
 
         interleave(nc.scalar.copy, dx_bf[1], dx_raw[0], P, HALF, P)
         interleave(nc.vector.tensor_copy, dx_bf[0], dx_raw[0], 0, P)
@@ -156,141 +159,151 @@ def tile_rows_pl_tnrownorm_kernel(tc, x, w1, w2, gn, dx, og, base, out_0, out_1,
         for b in range(2, 4):
             quantize(dx_q, dx_bf[b], P * b, P * (b + 1))
         for i in range(2):
-            product(tz1[i], w1_q, dx_q, i)
+            product(tz1, w1_q, dx_q, i)
+
         interleave(nc.vector.tensor_copy, w2_bf[0], w2_raw, 0, P)
         inverse(0)
         quantize(w2_q, w2_bf[0], 0, P)
         for i in range(2):
-            product(z2[i], w2_q, x_q, i)
-            product(tz2[i], w2_q, dx_q, i)
+            product(z2, w2_q, x_q, i)
+            product(tz2, w2_q, dx_q, i)
         row_stats(1)
-        for i in range(2):
-            sigmoid(i)
-            product(z1[i + 2], w1_q, x_q, i + 2)
         interleave(nc.scalar.copy, w2_bf[1], w2_raw, P, M, P)
-
-        halves = [slice(0, HALF), slice(HALF, N)]
-        plane_raw = [sb.tile([P, PACK, HALF], F32, name="plane_raw%d" % h, align_bytes=64) for h in range(2)]
-        plane_bf = [sb.tile([P, PACK * HALF], BF16, name="plane_bf%d" % h, align_bytes=64) for h in range(2)]
-        plane_codes = [sb.tile([P, HALF], U32, name="plane_codes%d" % h, align_bytes=64) for h in range(2)]
-        plane_scales = sb.tile([P, HALF], U8, align_bytes=64)
-        words = out_1.rearrange("s p n u -> (s p) (n u)").bitcast(I32).rearrange("(g h q) n -> h g q n", g=G, h=2)
-        scale_rows = out_2.rearrange("s f n -> (s f) n").bitcast(I32)
-
-        every = slice(0, N)
+        for i in range(2):
+            half_tanh(i)
+            product(z1, w1_q, x_q, i + 2)
 
         def step_kappa(i):
             nc.vector.scalar_tensor_tensor(
-                out=inner[i][:], in0=z1_mean[i][:], scalar=inv_ms[:, i : i + 1], in1=tz1[i][:],
-                op0=ALU.mult, op1=ALU.mult, accum_out=kappa[:, i : i + 1],
+                out=inner[i][:], in0=z1_scaled[i][:], scalar=inv_four_ms[:, i : i + 1], in1=tz1[i][:],
+                op0=ALU.mult, op1=ALU.mult, accum_out=two_kappa[:, i : i + 1],
             )
 
-        def step_slope(i):
+        def step_slope(i, cols=every):
             nc.vector.scalar_tensor_tensor(
-                out=slope[i][:], in0=gate[i][:], scalar=1.0, in1=tz2[i][:], op0=ALU.subtract, op1=ALU.mult
+                out=slope[i][:, cols], in0=th[i][:, cols], scalar=1.0, in1=tz2[i][:, cols],
+                op0=ALU.subtract, op1=ALU.mult,
             )
 
-        def step_cross(i):
+        def step_cross(i, cols=every):
             nc.vector.scalar_tensor_tensor(
-                out=cross[i][:], in0=slope[i][:], scalar=kappa[:, i : i + 1], in1=z1[i][:], op0=ALU.add, op1=ALU.mult
+                out=cross[i][:, cols], in0=slope[i][:, cols], scalar=two_kappa[:, i : i + 1], in1=z1[i][:, cols],
+                op0=ALU.add, op1=ALU.mult,
             )
 
-        def step_inner(i):
-            nc.vector.tensor_tensor(out=inner[i][:], in0=cross[i][:], in1=tz1[i][:], op=ALU.subtract)
-            if i < 2:
-                product(tz2[i + 2], w2_q, dx_q, i + 2)
-
-        def step_change(i, cols=every):
+        def step_inner(i, cols=every):
             nc.vector.scalar_tensor_tensor(
-                out=change[i][:, cols], in0=inner[i][:, cols], scalar=amp[:, i : i + 1], in1=gate[i][:, cols],
-                op0=ALU.mult, op1=ALU.mult,
+                out=inner[i][:, cols], in0=cross[i][:, cols], scalar=-0.5, in1=tz1[i][:, cols],
+                op0=ALU.mult, op1=ALU.add,
             )
 
-        def step_y(i, cols=every):
+        def step_gate(i):
+            nc.vector.scalar_tensor_tensor(
+                out=change[i][:], in0=th[i][:], scalar=1.0, in1=inner[i][:], op0=ALU.add, op1=ALU.mult
+            )
+
+        def step_result(target, i, cols=every):
             g, h = TILES[i]
-            nc.vector.tensor_tensor(out=y[i][:, cols], in0=base_sb[:, 2 * g + h, cols], in1=change[i][:, cols], op=ALU.subtract)
+            nc.vector.scalar_tensor_tensor(
+                out=target[:, cols], in0=change[i][:, cols], scalar=amp[h][:, g : g + 1], in1=base_sb[:, 2 * g + h, cols],
+                op0=ALU.mult, op1=ALU.add,
+            )
 
-        def regroup(i, queues):
+        def in_halves(step, *args):
+            for cols in halves:
+                step(*args, cols)
+
+        set_raw = [sb.tile([P, PACK, HALF], (F32, BF16)[h], name="set_raw%d" % h, align_bytes=64) for h in range(2)]
+        set_bf = tiles("set_bf", 2, [P, PACK * HALF], BF16)
+        set_codes = tiles("set_codes", 2, [P, HALF], U32)
+        set_scales = sb.tile([P, HALF], U8, align_bytes=64)
+        words = out_1.rearrange("s p n u -> (s p) (n u)").bitcast(I32).rearrange("(g h q) n -> h g q n", g=G, h=2)
+        scale_rows = out_2.rearrange("s f n -> (s f) n").bitcast(I32)
+
+        def regroup(source, i, queues):
             g, h = TILES[i]
             for c in range(2):
-                first = 64 * c + 32 * g
-                queues[c].dma_start(out=plane_raw[h][first : first + 32, :, :], in_=y[i][:, halves[c]])
+                first = QUADRANT * (2 * c + g)
+                queues[c].dma_start(out=set_raw[h][first : first + QUADRANT, :, :], in_=source[:, halves[c]])
 
         def store(i):
             g, h = TILES[i]
             row = M * g + P * h
             nc.sync.dma_start(out=out_0[row : row + P, :], in_=y[i][:])
 
-        def quantize_plane(h, queues):
-            nc.vector.quantize_mx(
-                out=plane_codes[h][:].bitcast(FP8X4), scales=plane_scales[4 * h : P, :], in_=plane_bf[h][:]
-            )
+        def quantize_set(h, queues):
+            nc.vector.quantize_mx(out=set_codes[h][:].bitcast(FP8X4), scales=set_scales[4 * h : P, :], in_=set_bf[h][:])
             for c in range(2):
                 queues[c].dma_start(
-                    out=words[h][:, :, halves[c]], in_=plane_codes[h][64 * c : 64 * (c + 1), :].bitcast(I32)
+                    out=words[h][:, :, halves[c]], in_=set_codes[h][ROWS * c : ROWS * (c + 1), :].bitcast(I32)
                 )
 
         step_kappa(0)
         inverse(1)
         nc.vector.transpose(out=gain_cols[:], in_=gain_rows[:])
         by_tile = gain_cols[:].rearrange("p (g h e) -> p h g e", g=G, h=2)
+        inverse_roots(0)
         nc.gpsimd.tensor_tensor(
             out=gains[:].rearrange("p (h g) -> p h g", g=G), in0=by_tile[:, :, :, 0], in1=by_tile[:, :, :, 1], op=ALU.mult
         )
-        amplitudes((0, 1))
+        nc.gpsimd.tensor_tensor(out=amp[0][:], in0=inv_two_rm[:, 0:G], in1=gains[:, 0:G], op=ALU.mult)
         step_kappa(1)
-        step_slope(0)
-        step_slope(1)
-        step_cross(0)
         quantize(w2_q, w2_bf[1], P, M)
-        step_cross(1)
-        for i in range(2, 4):
-            product(z2[i], w2_q, x_q, i)
-            product(tz1[i], w1_q, dx_q, i)
-        row_stats(2)
-        row_stats(3)
-        amplitudes((2, 3))
-        sigmoid(2)
-        sigmoid(3)
-        for step in (step_inner, step_change):
-            step(0)
-            step(1)
-        step_y(0)
-        regroup(0, [nc.sync, nc.sync])
-        store(0)
-        inverse(2)
-        step_y(1)
-        regroup(1, [nc.sync, nc.sync])
-        store(1)
-        inverse(3)
+        for i in range(2):
+            nc.gpsimd.tensor_scalar(
+                out=gate_amp[i][:], in0=th[i][:], scalar1=1.0, scalar2=amp[0][:, i : i + 1], op0=ALU.add, op1=ALU.mult
+            )
+
+        for i in range(2):
+            in_halves(step_slope, i)
+            product(z2, w2_q, x_q, i + 2)
+            in_halves(step_cross, i)
+            product(tz1, w1_q, dx_q, i + 2)
+            if i == 1:
+                inverse(2)
+            in_halves(step_inner, i)
+            product(tz2, w2_q, dx_q, i + 2)
+            row_stats(i + 2)
+            half_tanh(i + 2)
+            nc.gpsimd.tensor_tensor(out=change[i][:], in0=inner[i][:], in1=gate_amp[i][:], op=ALU.mult)
+            if i == 1:
+                inverse_roots(1)
+            nc.gpsimd.tensor_tensor(out=y[i][:], in0=change[i][:], in1=base_sb[:, 2 * i, :], op=ALU.add)
+            regroup(y[i], i, [nc.sync, nc.sync])
+            store(i)
+        for g in range(G):
+            col = slice(G + g, G + g + 1)
+            nc.scalar.activation(out=amp[1][:, g : g + 1], in_=inv_two_rm[:, col], func=ACT.Copy, scale=gains[:, col])
+
         step_kappa(2)
+        inverse(3)
         step_slope(2)
         step_kappa(3)
         step_cross(2)
         step_slope(3)
         step_inner(2)
-        step_cross(3)
-        step_change(2)
-        step_inner(3)
-        step_y(2)
-        interleave(nc.scalar.copy, plane_bf[0], plane_raw[0], 0, HALF)
-        regroup(2, [nc.sync, nc.scalar])
-        for cols in halves:
-            step_change(3, cols)
-        for cols in halves:
-            step_y(3, cols)
-        regroup(3, [nc.sync, nc.scalar])
-        store(2)
-        store(3)
-        quantize_plane(0, [nc.scalar, nc.scalar])
-        interleave(nc.vector.tensor_copy, plane_bf[1], plane_raw[1], 0, PLANE_SPLIT)
-        interleave(nc.scalar.copy, plane_bf[1], plane_raw[1], PLANE_SPLIT, HALF)
-        quantize_plane(1, [nc.sync, nc.scalar])
+        in_halves(step_cross, 3)
+        in_halves(step_inner, 3)
+        step_gate(2)
+        step_gate(3)
+        step_result(y_bf[0], 2)
+        regroup(y_bf[0], 2, [nc.sync, nc.scalar])
+        in_halves(step_result, y_bf[1], 3)
+        regroup(y_bf[1], 3, [nc.sync, nc.scalar])
+
+        interleave(nc.scalar.copy, set_bf[0], set_raw[0], 0, HALF)
+        for i in range(2, 4):
+            step_result(y[i], i)
+            store(i)
+        quantize_set(0, [nc.sync, nc.sync])
+        interleave(nc.vector.tensor_copy, set_bf[1], set_raw[1], 0, SET_SPLIT)
+        interleave(nc.scalar.copy, set_bf[1], set_raw[1], SET_SPLIT, HALF)
+        quantize_set(1, [nc.sync, nc.scalar])
+        words_in_half = HALF // 4
         for c in range(2):
             for g in range(G):
-                first = 64 * c + 32 * g
-                queue = nc.sync if g == 0 else nc.scalar
-                queue.dma_start(
-                    out=scale_rows[8 * g : 8 * (g + 1), 64 * c : 64 * (c + 1)],
-                    in_=plane_scales[first : first + 8, :].bitcast(I32),
+                first = QUADRANT * (2 * c + g)
+                (nc.sync, nc.scalar)[g].dma_start(
+                    out=scale_rows[8 * g : 8 * (g + 1), words_in_half * c : words_in_half * (c + 1)],
+                    in_=set_scales[first : first + 8, :].bitcast(I32),
                 )

from contextlib import ExitStack

import concourse.mybir as mybir

G, D, M, N = 2, 256, 256, 512
FLOPS = 4 * 2 * G * D * M * N

F32 = mybir.dt.float32
BF16 = mybir.dt.bfloat16
I32 = mybir.dt.int32
U32 = mybir.dt.uint32
U8 = mybir.dt.uint8
FP8X4 = mybir.dt.float8_e4m3fn_x4
ACT = mybir.ActivationFunctionType
ALU = mybir.AluOpType

P = 128
PACK = 4
ROWS = D // PACK
QUADRANT = 32
HALF = N // 2
EPS = 0.01
TILES = [(0, 0), (1, 0), (0, 1), (1, 1)]
X_SPLIT = 336
SET_SPLIT = 160


def interleave(copy, grouped, raw, first, last, origin=0):
    run = 2 if raw.dtype == F32 else 4
    target = grouped[:, PACK * (first - origin) : PACK * (last - origin)]
    copy(
        out=target.rearrange("p (c i t) -> p c t i", i=run, t=PACK),
        in_=raw[:, :, first:last].rearrange("p t (c i) -> p c t i", i=run),
    )


def tile_rows_pl_tnrownorm_kernel(tc, x, w1, w2, gn, dx, og, base, out_0, out_1, out_2):
    nc = tc.nc
    with ExitStack() as ctx:
        sb = ctx.enter_context(tc.tile_pool(name="sb", bufs=1))
        ps = ctx.enter_context(tc.psum_pool(name="ps", bufs=1))
        ctx.enter_context(tc.manual_schedule())

        def tiles(name, count, shape, dtype):
            return [sb.tile(shape, dtype, name="%s%d" % (name, i), align_bytes=64) for i in range(count)]

        def mx_operand(name, width):
            codes = sb.tile([P, width], U32, name=name + "_codes", align_bytes=64)
            scales = sb.tile([P, width], U8, name=name + "_scales", align_bytes=64)
            return codes, scales

        def quantize(operand, grouped, first, last):
            codes, scales = operand
            nc.vector.quantize_mx(out=codes[:, first:last].bitcast(FP8X4), scales=scales[:, first:last], in_=grouped[:])

        def product(banks_by_tile, weights, moving, i):
            g, h = TILES[i]
            rows = slice(ROWS * g, ROWS * (g + 1))
            features = slice(P * h, P * (h + 1))
            nc.tensor.matmul_mx(
                out=banks_by_tile[i][:],
                lhsT=weights[0][rows, features].bitcast(FP8X4),
                lhsT_scale=weights[1][rows, features],
                rhs=moving[0][rows, :].bitcast(FP8X4),
                rhs_scale=moving[1][rows, :],
                start=True,
                stop=True,
            )

        banks = [[ps.tile([P, N], F32, name="bank%d_%d" % (g, b)) for b in range(4)] for g in range(G)]
        z1 = [banks[g][(0, 1)[h]] for g, h in TILES]
        z2 = [banks[g][(1, 3)[h]] for g, h in TILES]
        tz1 = [banks[g][(2, 0)[h]] for g, h in TILES]
        tz2 = [banks[g][(3, 2)[h]] for g, h in TILES]

        w1_raw = sb.tile([P, PACK, M], F32, align_bytes=64)
        w2_raw = sb.tile([P, PACK, M], F32, align_bytes=64)
        x_raw = sb.tile([P, PACK, N], F32, align_bytes=64)
        dx_raw = tiles("dx_raw", 2, [P, PACK, HALF], F32)
        gain_rows = sb.tile([P, QUADRANT], F32, align_bytes=64)
        gain_cols = sb.tile([P, QUADRANT], F32, align_bytes=64)
        base_sb = sb.tile([P, len(TILES), N], F32, align_bytes=64)
        halves = [slice(0, HALF), slice(HALF, N)]
        every = slice(0, N)
        packed_rows = "g (p j) n -> (g p) j n"
        nc.vector.memset(gain_rows[:], 0.0)
        nc.sync.dma_start(out=x_raw[:], in_=x.rearrange(packed_rows, j=PACK))
        nc.sync.dma_start(out=w1_raw[:], in_=w1.rearrange(packed_rows, j=PACK))
        for c in range(2):
            nc.sync.dma_start(out=dx_raw[c][:], in_=dx.rearrange(packed_rows, j=PACK)[:, :, halves[c]])
        nc.sync.dma_start(out=w2_raw[:], in_=w2.rearrange(packed_rows, j=PACK))
        for e, gain in enumerate((gn, og)):
            nc.sync.dma_start(out=gain_rows[e:P:8, :], in_=gain.rearrange("g (h q r) o -> q (g h) (r o)", h=2, q=4))
        nc.sync.dma_start(out=base_sb[:], in_=base.rearrange("g (h p) n -> p (g h) n", p=P))

        th = tiles("th", len(TILES), [P, N], F32)
        gate_amp = tiles("gate_amp", 2, [P, N], F32)
        z1_scaled = tiles("z1_scaled", len(TILES), [P, N], F32)
        slope = tiles("slope", len(TILES), [P, N], F32)
        cross = tiles("cross", len(TILES), [P, N], F32)
        inner = tiles("inner", len(TILES), [P, N], F32)
        change = tiles("change", len(TILES), [P, N], F32)
        y = tiles("y", len(TILES), [P, N], F32)
        y_bf = tiles("y_bf", 2, [P, N], BF16)
        sum_sq = sb.tile([P, len(TILES)], F32)
        four_ms = sb.tile([P, len(TILES)], F32)
        inv_four_ms = sb.tile([P, len(TILES)], F32)
        two_kappa = sb.tile([P, len(TILES)], F32)
        inv_two_rm = sb.tile([P, len(TILES)], F32)
        gains = sb.tile([P, len(TILES)], F32)
        amp = tiles("amp", 2, [P, 2], F32)
        minus_half = sb.tile([P, 2], F32)
        nc.gpsimd.memset(minus_half[:], -0.5)

        def row_stats(i):
            col = slice(i, i + 1)
            nc.scalar.activation(out=th[i][:], in_=z1[i][:], func=ACT.Square, accum_out=sum_sq[:, col])
            nc.scalar.activation(out=z1_scaled[i][:], in_=z1[i][:], func=ACT.Copy, scale=8.0 / N)
            nc.scalar.activation(out=four_ms[:, col], in_=sum_sq[:, col], func=ACT.Identity, scale=4.0 / N, bias=4.0 * EPS)

        def half_tanh(i):
            nc.scalar.activation(out=th[i][:], in_=z2[i][:], func=ACT.Tanh, scale=0.5)

        def inverse(i):
            nc.vector.reciprocal(out=inv_four_ms[:, i : i + 1], in_=four_ms[:, i : i + 1])

        def inverse_roots(h):
            cols = slice(G * h, G * (h + 1))
            nc.gpsimd.tensor_tensor(out=inv_two_rm[:, cols], in0=four_ms[:, cols], in1=minus_half[:], op=ALU.pow)

        w1_q = mx_operand("w1", M)
        w2_q = mx_operand("w2", M)
        x_q = mx_operand("x", N)
        dx_q = mx_operand("dx", N)
        w1_bf = tiles("w1_bf", 2, [P, PACK * P], BF16)
        w2_bf = tiles("w2_bf", 2, [P, PACK * P], BF16)
        x_bf = tiles("x_bf", 2, [P, PACK * HALF], BF16)
        dx_bf = tiles("dx_bf", 4, [P, PACK * P], BF16)

        interleave(nc.vector.tensor_copy, x_bf[0], x_raw, 0, HALF)
        interleave(nc.scalar.copy, x_bf[1], x_raw, X_SPLIT, N, HALF)
        interleave(nc.vector.tensor_copy, x_bf[1], x_raw, HALF, X_SPLIT, HALF)
        for c in range(2):
            quantize(x_q, x_bf[c], HALF * c, HALF * (c + 1))
        interleave(nc.scalar.copy, w1_bf[0], w1_raw, 0, P)
        interleave(nc.vector.tensor_copy, w1_bf[1], w1_raw, P, M, P)
        for h in range(2):
            quantize(w1_q, w1_bf[h], P * h, P * (h + 1))
        for i in range(2):
            product(z1, w1_q, x_q, i)

        interleave(nc.scalar.copy, dx_bf[1], dx_raw[0], P, HALF, P)
        interleave(nc.vector.tensor_copy, dx_bf[0], dx_raw[0], 0, P)
        for b in range(2):
            quantize(dx_q, dx_bf[b], P * b, P * (b + 1))
        row_stats(0)
        for b in range(2):
            interleave(nc.vector.tensor_copy, dx_bf[2 + b], dx_raw[1], P * b, P * (b + 1), P * b)
        for b in range(2, 4):
            quantize(dx_q, dx_bf[b], P * b, P * (b + 1))
        for i in range(2):
            product(tz1, w1_q, dx_q, i)

        interleave(nc.vector.tensor_copy, w2_bf[0], w2_raw, 0, P)
        inverse(0)
        quantize(w2_q, w2_bf[0], 0, P)
        for i in range(2):
            product(z2, w2_q, x_q, i)
            product(tz2, w2_q, dx_q, i)
        row_stats(1)
        interleave(nc.scalar.copy, w2_bf[1], w2_raw, P, M, P)
        for i in range(2):
            half_tanh(i)
            product(z1, w1_q, x_q, i + 2)

        def step_kappa(i):
            nc.vector.scalar_tensor_tensor(
                out=inner[i][:], in0=z1_scaled[i][:], scalar=inv_four_ms[:, i : i + 1], in1=tz1[i][:],
                op0=ALU.mult, op1=ALU.mult, accum_out=two_kappa[:, i : i + 1],
            )

        def step_slope(i, cols=every):
            nc.vector.scalar_tensor_tensor(
                out=slope[i][:, cols], in0=th[i][:, cols], scalar=1.0, in1=tz2[i][:, cols],
                op0=ALU.subtract, op1=ALU.mult,
            )

        def step_cross(i, cols=every):
            nc.vector.scalar_tensor_tensor(
                out=cross[i][:, cols], in0=slope[i][:, cols], scalar=two_kappa[:, i : i + 1], in1=z1[i][:, cols],
                op0=ALU.add, op1=ALU.mult,
            )

        def step_inner(i, cols=every):
            nc.vector.scalar_tensor_tensor(
                out=inner[i][:, cols], in0=cross[i][:, cols], scalar=-0.5, in1=tz1[i][:, cols],
                op0=ALU.mult, op1=ALU.add,
            )

        def step_gate(i):
            nc.vector.scalar_tensor_tensor(
                out=change[i][:], in0=th[i][:], scalar=1.0, in1=inner[i][:], op0=ALU.add, op1=ALU.mult
            )

        def step_result(target, i, cols=every):
            g, h = TILES[i]
            nc.vector.scalar_tensor_tensor(
                out=target[:, cols], in0=change[i][:, cols], scalar=amp[h][:, g : g + 1], in1=base_sb[:, 2 * g + h, cols],
                op0=ALU.mult, op1=ALU.add,
            )

        def in_halves(step, *args):
            for cols in halves:
                step(*args, cols)

        set_raw = [sb.tile([P, PACK, HALF], (F32, BF16)[h], name="set_raw%d" % h, align_bytes=64) for h in range(2)]
        set_bf = tiles("set_bf", 2, [P, PACK * HALF], BF16)
        set_codes = tiles("set_codes", 2, [P, HALF], U32)
        set_scales = sb.tile([P, HALF], U8, align_bytes=64)
        words = out_1.rearrange("s p n u -> (s p) (n u)").bitcast(I32).rearrange("(g h q) n -> h g q n", g=G, h=2)
        scale_rows = out_2.rearrange("s f n -> (s f) n").bitcast(I32)

        def regroup(source, i, queues):
            g, h = TILES[i]
            for c in range(2):
                first = QUADRANT * (2 * c + g)
                queues[c].dma_start(out=set_raw[h][first : first + QUADRANT, :, :], in_=source[:, halves[c]])

        def store(i):
            g, h = TILES[i]
            row = M * g + P * h
            nc.sync.dma_start(out=out_0[row : row + P, :], in_=y[i][:])

        def quantize_set(h, queues):
            nc.vector.quantize_mx(out=set_codes[h][:].bitcast(FP8X4), scales=set_scales[4 * h : P, :], in_=set_bf[h][:])
            for c in range(2):
                queues[c].dma_start(
                    out=words[h][:, :, halves[c]], in_=set_codes[h][ROWS * c : ROWS * (c + 1), :].bitcast(I32)
                )

        step_kappa(0)
        inverse(1)
        nc.vector.transpose(out=gain_cols[:], in_=gain_rows[:])
        by_tile = gain_cols[:].rearrange("p (g h e) -> p h g e", g=G, h=2)
        inverse_roots(0)
        nc.gpsimd.tensor_tensor(
            out=gains[:].rearrange("p (h g) -> p h g", g=G), in0=by_tile[:, :, :, 0], in1=by_tile[:, :, :, 1], op=ALU.mult
        )
        nc.gpsimd.tensor_tensor(out=amp[0][:], in0=inv_two_rm[:, 0:G], in1=gains[:, 0:G], op=ALU.mult)
        step_kappa(1)
        quantize(w2_q, w2_bf[1], P, M)
        for i in range(2):
            nc.gpsimd.tensor_scalar(
                out=gate_amp[i][:], in0=th[i][:], scalar1=1.0, scalar2=amp[0][:, i : i + 1], op0=ALU.add, op1=ALU.mult
            )

        for i in range(2):
            in_halves(step_slope, i)
            product(z2, w2_q, x_q, i + 2)
            in_halves(step_cross, i)
            product(tz1, w1_q, dx_q, i + 2)
            if i == 1:
                inverse(2)
            in_halves(step_inner, i)
            product(tz2, w2_q, dx_q, i + 2)
            row_stats(i + 2)
            half_tanh(i + 2)
            nc.gpsimd.tensor_tensor(out=change[i][:], in0=inner[i][:], in1=gate_amp[i][:], op=ALU.mult)
            if i == 1:
                inverse_roots(1)
            nc.gpsimd.tensor_tensor(out=y[i][:], in0=change[i][:], in1=base_sb[:, 2 * i, :], op=ALU.add)
            regroup(y[i], i, [nc.sync, nc.sync])
            store(i)
        for g in range(G):
            col = slice(G + g, G + g + 1)
            nc.scalar.activation(out=amp[1][:, g : g + 1], in_=inv_two_rm[:, col], func=ACT.Copy, scale=gains[:, col])

        step_kappa(2)
        inverse(3)
        step_slope(2)
        step_kappa(3)
        step_cross(2)
        step_slope(3)
        step_inner(2)
        in_halves(step_cross, 3)
        in_halves(step_inner, 3)
        step_gate(2)
        step_gate(3)
        step_result(y_bf[0], 2)
        regroup(y_bf[0], 2, [nc.sync, nc.scalar])
        in_halves(step_result, y_bf[1], 3)
        regroup(y_bf[1], 3, [nc.sync, nc.scalar])

        interleave(nc.scalar.copy, set_bf[0], set_raw[0], 0, HALF)
        for i in range(2, 4):
            step_result(y[i], i)
            store(i)
        quantize_set(0, [nc.sync, nc.sync])
        interleave(nc.vector.tensor_copy, set_bf[1], set_raw[1], 0, SET_SPLIT)
        interleave(nc.scalar.copy, set_bf[1], set_raw[1], SET_SPLIT, HALF)
        quantize_set(1, [nc.sync, nc.scalar])
        words_in_half = HALF // 4
        for c in range(2):
            for g in range(G):
                first = QUADRANT * (2 * c + g)
                (nc.sync, nc.scalar)[g].dma_start(
                    out=scale_rows[8 * g : 8 * (g + 1), words_in_half * c : words_in_half * (c + 1)],
                    in_=set_scales[first : first + 8, :].bitcast(I32),
                )
